import numpy as np
import ml_dtypes


def mxq(x, axis, fmt="e4m3"):
    dtype, down = {"e4m3": (ml_dtypes.float8_e4m3fn, 7), "e5m2": (ml_dtypes.float8_e5m2, 14)}[fmt]
    v = np.moveaxis(np.asarray(x, np.float32).astype(ml_dtypes.bfloat16).astype(np.float64), axis, -1)
    blocks = v.reshape(v.shape[:-1] + (-1, 32))
    amax = np.abs(blocks).max(-1, keepdims=True)
    byte = np.maximum(np.where(amax > 0, np.frexp(amax)[1] - 1 + 127, 0) - down, 1)
    scale = np.exp2(byte - 127.0)
    codes = (blocks / scale).astype(np.float32).astype(dtype).astype(np.float64)
    return np.moveaxis((codes * scale).reshape(v.shape), -1, axis)


WIDE = False


def mx_kscale(k):
    if not WIDE:
        return np.ones(k)
    levels = np.array([10, -10, 5, -5, 0])
    if k % 512:
        return np.exp2(np.random.permutation(np.resize(levels, k // 32))).repeat(32)
    a = np.empty((k // 512, 16))
    for p in range(k // 512):
        a[p, :8] = np.random.permutation(np.resize(levels, 8))
        for g in range(8):
            far = levels[np.abs(levels - a[p, g]) >= 10]
            a[p, g + 8] = far[np.random.randint(len(far))]
    return np.exp2(a.ravel()).repeat(32)


def f64(x):
    return np.asarray(x).astype(np.float64)


def striped(idx):
    return np.tile(np.asarray(idx).reshape(-1, 16).T, (8, 1)).astype(np.uint16)


def unstriped(offs):
    return offs[:16].T.reshape(-1).astype(np.int64)


E2M1 = np.array([0.0, 0.5, 1.0, 1.5, 2.0, 3.0, 4.0, 6.0, -0.0, -0.5, -1.0, -1.5, -2.0, -3.0, -4.0, -6.0])


def pack_weight(w, fmt):
    k, n = w.shape
    w = f64(np.asarray(w, np.float32).astype(ml_dtypes.bfloat16)).reshape(k // 32, 32, n)
    amax = np.abs(w).max(1)
    if fmt == "e4m3":
        byte = np.frexp(amax)[1] - 1 + 127 - 7
    else:
        mant, ex = np.frexp(amax / 6.0)
        byte = np.where(mant > 0.5, ex, ex - 1) + 127
    byte = np.clip(np.where(amax > 0, byte, 1), 1, 254)
    scaled = (w * np.exp2(127.0 - byte)[:, None, :]).reshape(k, n).astype(np.float32)
    by_word = np.ascontiguousarray(scaled.reshape(k // 512, 128, 4, n).transpose(0, 1, 3, 2))
    if fmt == "e4m3":
        words = by_word.astype(ml_dtypes.float8_e4m3fn).view(np.uint8)
    else:
        c = by_word.astype(ml_dtypes.float4_e2m1fn).view(np.uint8) & 0xF
        words = (c[..., 0::2] | (c[..., 1::2] << 4)).reshape(k // 512, 128, 2 * n)
    return np.ascontiguousarray(words), np.ascontiguousarray(byte.astype(np.uint8).reshape(k // 512, 16, n))


def unpack_weight(words, scales, fmt):
    g, _, n = scales.shape
    words = np.ascontiguousarray(words).reshape(g, 128, n, -1)
    if fmt == "e4m3":
        vals = words.view(ml_dtypes.float8_e4m3fn).astype(np.float64)
    else:
        nib = np.empty((g, 128, n, 4), np.uint8)
        nib[..., 0::2] = words & 0xF
        nib[..., 1::2] = words >> 4
        vals = E2M1[nib]
    vals = vals * np.repeat(np.exp2(scales.astype(np.float64) - 127.0), 8, axis=1)[..., None]
    return vals.transpose(0, 1, 3, 2).reshape(g * 512, n)


def gelu(v):
    return 0.5 * v * (1.0 + np.tanh(0.7978845608028654 * (v + 0.044715 * v ** 3)))


def bf(x):
    return np.asarray(x, np.float32).astype(ml_dtypes.bfloat16)


def planes(Y):
    r, m = Y.shape
    b = f64(bf(Y)).reshape(r // 32, 32, m)
    amax = np.abs(b).max(1)
    byte = np.clip(np.where(amax > 0, np.frexp(amax)[1] - 1 + 127 - 7, 1), 1, 254)
    codes = (b * np.exp2(127.0 - byte)[:, None, :]).reshape(r, m).astype(np.float32).astype(ml_dtypes.float8_e4m3fn).view(np.uint8)
    words = codes.reshape(r // 512, 128, 4, m).transpose(0, 1, 3, 2)
    return np.ascontiguousarray(words), np.ascontiguousarray(byte.astype(np.uint8).reshape(r // 512, 16, m))


K, T, J, F, D = 512, 2048, 512, 512, 512


def setup_inputs():
    n = np.random.standard_normal
    idx = np.random.permutation(T)[:J]
    idx2 = np.random.permutation(T)[:J]
    idx3 = np.random.permutation(T)[:J]
    idx4 = np.random.permutation(T)[:J]
    fk = mx_kscale(K)
    ff = mx_kscale(F)
    tokp = pack_weight(n((K, T)) / fk[:, None], "e4m3")
    return {
        "tok_words": tokp[0],
        "tok_scales": tokp[1],
        "w0": (n((K, F)) * 0.5 / np.sqrt(K) * fk[:, None]).astype(np.float32),
        "w1": (n((K, F)) * 0.5 / np.sqrt(K) * fk[:, None]).astype(np.float32),
        "w2": (n((K, F)) * 0.5 / np.sqrt(K) * fk[:, None]).astype(np.float32),
        "w3": (n((K, F)) * 0.5 / np.sqrt(K) * fk[:, None]).astype(np.float32),
        "gain": (np.random.uniform(0.5, 2.0, (F, 1)) * ff[:, None]).astype(np.float32),
        "wo": (n((F, D)) * 1 / np.sqrt(F) / ff[:, None]).astype(np.float32),
        "offs": striped(idx),
        "offs2": striped(idx2),
        "offs3": striped(idx3),
        "offs4": striped(idx4),
    }


def reference(tok_words, tok_scales, w0, w1, w2, w3, gain, wo, offs, offs2, offs3, offs4):
    idx = unstriped(offs)
    idx2 = unstriped(offs2)
    idx3 = unstriped(offs3)
    idx4 = unstriped(offs4)
    toku = unpack_weight(tok_words, tok_scales, "e4m3")
    w0q = mxq(f64(w0), 0, "e4m3")
    tokidxg = toku[:, idx]
    w1q = mxq(f64(w1), 0, "e4m3")
    tokidx2g = toku[:, idx2]
    w2q = mxq(f64(w2), 0, "e4m3")
    tokidx3g = toku[:, idx3]
    w3q = mxq(f64(w3), 0, "e4m3")
    tokidx4g = toku[:, idx4]
    z = w0q.T @ tokidxg + w1q.T @ tokidx2g + w2q.T @ tokidx3g + w3q.T @ tokidx4g
    g = gelu(z) * f64(gain)
    woq = mxq(f64(wo), 0, "e4m3")
    gq = mxq(g, 0, "e4m3")
    y = woq.T @ gq
    words, scales = planes(y)
    return y, words, scales

@@ -1,0 +1,176 @@
+from contextlib import ExitStack
+
+import concourse.mybir as mybir
+
+F32 = mybir.dt.float32
+BF16 = mybir.dt.bfloat16
+I32 = mybir.dt.int32
+U32 = mybir.dt.uint32
+U16 = mybir.dt.uint16
+U8 = mybir.dt.uint8
+FP8X4 = mybir.dt.float8_e4m3fn_x4
+GELU = mybir.ActivationFunctionType.Gelu_apprx_tanh
+MULT = mybir.AluOpType.mult
+
+P = 128
+PACK = 4
+K, T, J, F, D = 512, 2048, 512, 512, 512
+GELU_CHUNKS = [256, 256]
+CHUNKS = [128, 128, 128, 128]
+Y_STORES = [256, 128, 128]
+WORD_STORES = [384, 128]
+SPLIT3 = 68
+SPLITO = 0
+OVERLAP = 32
+FLOPS = 2 * (4 * K * F * J + F * D * J)
+
+
+def spans(widths):
+    return [(sum(widths[:c]), widths[c]) for c in range(len(widths))]
+
+
+def tile_attend_nsa_compress_pl_kernel(tc, tok_words, tok_scales, w0, w1, w2, w3, gain, wo,
+                                        offs, offs2, offs3, offs4, out_0, out_1, out_2):
+    nc = tc.nc
+    with ExitStack() as ctx:
+        keep = ctx.enter_context(tc.tile_pool(name="keep", bufs=1))
+        psum = ctx.enter_context(tc.psum_pool(name="psum", bufs=1))
+
+        def load_raw(name, w, queue):
+            raw = keep.tile([P, PACK, F], F32, name=name + "_raw", align_bytes=64)
+            queue.dma_start(out=raw[:], in_=w.rearrange("(p j) c -> p j c", j=PACK))
+            return raw
+
+        def deal(copy, grouped, raw, m0, m1):
+            copy(out=grouped.rearrange("p (t m j) -> p m j t", t=PACK, j=PACK)[:, m0:m1],
+                 in_=raw[:].rearrange("p j (m t) -> p m j t", t=PACK)[:, m0:m1])
+
+        def quantize(name, grouped, pieces):
+            codes = keep.tile([P, F], U32, name=name + "_codes", align_bytes=64)
+            scales = keep.tile([P, F], U8, name=name + "_scales", align_bytes=64)
+            n = F // pieces
+            for a in range(0, F, n):
+                nc.vector.quantize_mx(out=codes[:, a:a + n].bitcast(FP8X4), scales=scales[:, a:a + n],
+                                      in_=grouped[:, PACK * a:PACK * (a + n)])
+            return codes, scales
+
+        pool_scales = keep.tile([P, T], U8, name="pool_scales", align_bytes=64)
+        warm_in = keep.tile([P, 1], F32, name="warm_in")
+        warm_out = keep.tile([P, 1], F32, name="warm_out")
+        nc.vector.memset(warm_in[:], 0.0)
+        nc.scalar.activation(out=warm_out[:], in_=warm_in[:], func=GELU)
+
+        lists = [keep.tile([P, J // 16], U16, name="list%d" % i) for i in range(4)]
+        pool_words = keep.tile([P, T], U32, name="pool_words", align_bytes=64)
+        gain_sb = keep.tile([P, PACK], F32, name="gain_sb")
+
+        def load_scales(q, queue):
+            rows = tok_scales[0, 4 * q:4 * q + 4, :].bitcast(I32)
+            queue.dma_start(out=pool_scales[32 * q:32 * q + 32, :].bitcast(I32),
+                            in_=rows.unsqueeze(0).to_broadcast([8, 4, T // 4]))
+
+        def load_words(queue):
+            queue.dma_start(out=pool_words[:].bitcast(I32),
+                            in_=tok_words[0].rearrange("p n t -> p (n t)").bitcast(I32))
+
+        nc.sync.dma_start(lists[0][:], offs)
+        for q in range(4):
+            load_scales(q, nc.sync)
+        nc.sync.dma_start(lists[1][:], offs2)
+        nc.sync.dma_start(lists[2][:], offs3)
+        raws = [load_raw("w0", w0, nc.sync)]
+        nc.sync.dma_start(lists[3][:], offs4)
+        load_words(nc.sync)
+        for i, w in ((1, w1), (2, w2), (3, w3)):
+            raws.append(load_raw("w%d" % i, w, nc.sync))
+        nc.sync.dma_start(out=gain_sb[:], in_=gain.rearrange("(p t) o -> p (t o)", t=PACK))
+        wo_raw = load_raw("wo", wo, nc.sync)
+
+        tok_s = []
+        for i in range(4):
+            s = keep.tile([P, J], U8, name="tok_s%d" % i, align_bytes=64)
+            nc.vector.tensor_copy(out=s[:], in_=pool_scales[:].indirect(lists[i][:]))
+            tok_s.append(s)
+
+        z = [[psum.tile([P, w], F32, name="z%d_%d" % (h, t), tag="bank%d" % (PACK * h + t)) for t in range(PACK)]
+             for h, w in enumerate(GELU_CHUNKS)]
+        tok_w = []
+        for i in range(4):
+            g = keep.tile([P, J], U32, name="tok_w%d" % i, align_bytes=64)
+            nc.vector.tensor_copy(out=g[:], in_=pool_words[:].indirect(lists[i][:]))
+            tok_w.append(g)
+        width = F * PACK
+        bf01 = [keep.tile([P, width], BF16, name="w%d_bf" % i, align_bytes=64) for i in range(2)]
+        bf23 = keep.tile([P, 2 * width - OVERLAP], BF16, name="w23_bf", align_bytes=64)
+        groupeds = [bf01[0][:], bf01[1][:], bf23[:, width - OVERLAP:], bf23[:, :width]]
+        for i in range(4):
+            grouped = groupeds[i]
+            if i < 3:
+                deal(nc.scalar.copy, grouped, raws[i], 0, P)
+            else:
+                deal(nc.scalar.copy, grouped, raws[i], 0, SPLIT3)
+                deal(nc.vector.tensor_copy, grouped, raws[i], SPLIT3, P)
+            codes, scales = quantize("w%d" % i, grouped, 1)
+            for h, (j0, w) in enumerate(spans(GELU_CHUNKS)):
+                for t in range(PACK):
+                    cols = slice(t * P, (t + 1) * P)
+                    nc.tensor.matmul_mx(out=z[h][t][:], lhsT=codes[:, cols].bitcast(FP8X4),
+                                        lhsT_scale=scales[:, cols],
+                                        rhs=tok_w[i][:, j0:j0 + w].bitcast(FP8X4),
+                                        rhs_scale=tok_s[i][:, j0:j0 + w], start=(i == 0), stop=(i == 3))
+
+        wo_bf = keep.tile([P, width], BF16, name="wo_bf", align_bytes=64)
+        deal(nc.vector.tensor_copy, wo_bf[:], wo_raw, SPLITO, P)
+
+        act = keep.tile([P, PACK, J], F32, name="act", align_bytes=64)
+        for c, (j0, w) in enumerate(spans(GELU_CHUNKS)):
+            for t in range(PACK):
+                nc.scalar.activation(out=act[:, t, j0:j0 + w], in_=z[c][t][:], func=GELU)
+            if c == 0 and SPLITO > 0:
+                deal(nc.scalar.copy, wo_bf[:], wo_raw, 0, SPLITO)
+        wo_codes, wo_scales = quantize("wo", wo_bf[:], 1)
+
+        hidden = []
+        for c, (j0, w) in enumerate(spans(CHUNKS)):
+            g_bf = keep.tile([P, w * PACK], BF16, name="g_bf%d" % c, align_bytes=64)
+            nc.vector.tensor_tensor(
+                out=g_bf[:].rearrange("p (c i t) -> p c t i", i=4, t=PACK),
+                in0=act[:, :, j0:j0 + w].rearrange("p t (c i) -> p c t i", i=4),
+                in1=gain_sb[:].unsqueeze(1).unsqueeze(3).to_broadcast([P, w // 4, PACK, 4]),
+                op=MULT)
+            g_codes = keep.tile([P, w], U32, name="g_codes%d" % c, align_bytes=64)
+            g_scales = keep.tile([P, w], U8, name="g_scales%d" % c, align_bytes=64)
+            nc.vector.quantize_mx(out=g_codes[:].bitcast(FP8X4), scales=g_scales[:], in_=g_bf[:])
+            hidden.append((g_codes, g_scales))
+
+        y = keep.tile([P, PACK, J], F32, name="y", align_bytes=64)
+        y_codes = keep.tile([P, J], U32, name="y_codes", align_bytes=64)
+        y_scales = keep.tile([P, J], U8, name="y_scales", align_bytes=64)
+        out_rows = out_0.rearrange("(p t) j -> p t j", t=PACK)
+        out_words = out_1[0].rearrange("p n t -> p (n t)").bitcast(I32)
+        y_ends = {a + n: a for a, n in spans(Y_STORES)}
+        word_ends = {a + n: a for a, n in spans(WORD_STORES)}
+        for c, (j0, w) in enumerate(spans(CHUNKS)):
+            g_codes, g_scales = hidden[c]
+            bank = psum.tile([P, PACK, w], F32, name="ybank%d" % c, tag="bank%d" % c)
+            for t in range(PACK):
+                cols = slice(t * P, (t + 1) * P)
+                nc.tensor.matmul_mx(out=bank[:, t, :], lhsT=wo_codes[:, cols].bitcast(FP8X4),
+                                    lhsT_scale=wo_scales[:, cols], rhs=g_codes[:].bitcast(FP8X4),
+                                    rhs_scale=g_scales[:], start=True, stop=True)
+            nc.scalar.copy(out=y[:, :, j0:j0 + w], in_=bank[:])
+            if j0 + w in y_ends:
+                a = y_ends[j0 + w]
+                nc.sync.dma_start(out=out_rows[:, :, a:j0 + w], in_=y[:, :, a:j0 + w])
+            y_bf = keep.tile([P, w * PACK], BF16, name="y_bf%d" % c, align_bytes=64)
+            nc.vector.tensor_copy(out=y_bf[:].rearrange("p (c i t) -> p c t i", i=4, t=PACK),
+                                  in_=y[:, :, j0:j0 + w].rearrange("p t (c i) -> p c t i", i=4))
+            nc.vector.quantize_mx(out=y_codes[:, j0:j0 + w].bitcast(FP8X4), scales=y_scales[:, j0:j0 + w],
+                                  in_=y_bf[:])
+            if j0 + w in word_ends:
+                a = word_ends[j0 + w]
+                nc.sync.dma_start(out=out_words[:, a:j0 + w], in_=y_codes[:, a:j0 + w].bitcast(I32))
+        for q in range(4):
+            queue = nc.sync if q == 0 else nc.scalar
+            queue.dma_start(out=out_2[0, 4 * q:4 * q + 4, :].bitcast(I32),
+                            in_=y_scales[32 * q:32 * q + 4, :].bitcast(I32))

@@ -10,23 +10,17 @@ U16 = mybir.dt.uint16
 U8 = mybir.dt.uint8
 FP8X4 = mybir.dt.float8_e4m3fn_x4
 GELU = mybir.ActivationFunctionType.Gelu_apprx_tanh
+COPY = mybir.ActivationFunctionType.Copy
 MULT = mybir.AluOpType.mult
 
 P = 128
 PACK = 4
 K, T, J, F, D = 512, 2048, 512, 512, 512
-GELU_CHUNKS = [256, 256]
+HALF = J // 2
 CHUNKS = [128, 128, 128, 128]
-Y_STORES = [256, 128, 128]
-WORD_STORES = [384, 128]
-SPLIT3 = 68
-SPLITO = 0
-OVERLAP = 32
+GROUPS = [[0], [1], [2], [3]]
+WORD_STORES_AFTER = [2, 3]
 FLOPS = 2 * (4 * K * F * J + F * D * J)
-
-
-def spans(widths):
-    return [(sum(widths[:c]), widths[c]) for c in range(len(widths))]
 
 
 def tile_attend_nsa_compress_pl_kernel(tc, tok_words, tok_scales, w0, w1, w2, w3, gain, wo,
@@ -41,25 +35,21 @@ def tile_attend_nsa_compress_pl_kernel(tc, tok_words, tok_scales, w0, w1, w2, w3
             queue.dma_start(out=raw[:], in_=w.rearrange("(p j) c -> p j c", j=PACK))
             return raw
 
-        def deal(copy, grouped, raw, m0, m1):
-            copy(out=grouped.rearrange("p (t m j) -> p m j t", t=PACK, j=PACK)[:, m0:m1],
-                 in_=raw[:].rearrange("p j (m t) -> p m j t", t=PACK)[:, m0:m1])
+        def deal(copy, grouped, raw, t0, t1):
+            copy(out=grouped.rearrange("p (t m j) -> p m j t", t=t1 - t0, j=PACK),
+                 in_=raw[:].rearrange("p j (m t) -> p m j t", t=PACK)[:, :, :, t0:t1])
 
-        def quantize(name, grouped, pieces):
-            codes = keep.tile([P, F], U32, name=name + "_codes", align_bytes=64)
-            scales = keep.tile([P, F], U8, name=name + "_scales", align_bytes=64)
-            n = F // pieces
-            for a in range(0, F, n):
-                nc.vector.quantize_mx(out=codes[:, a:a + n].bitcast(FP8X4), scales=scales[:, a:a + n],
-                                      in_=grouped[:, PACK * a:PACK * (a + n)])
+        def mx_tiles(name, n):
+            codes = keep.tile([P, n], U32, name=name + "_codes", align_bytes=64)
+            scales = keep.tile([P, n], U8, name=name + "_scales", align_bytes=64)
             return codes, scales
+
+        def quantize(codes, scales, grouped):
+            nc.vector.quantize_mx(out=codes.bitcast(FP8X4), scales=scales, in_=grouped)
 
         pool_scales = keep.tile([P, T], U8, name="pool_scales", align_bytes=64)
         warm_in = keep.tile([P, 1], F32, name="warm_in")
         warm_out = keep.tile([P, 1], F32, name="warm_out")
-        nc.vector.memset(warm_in[:], 0.0)
-        nc.scalar.activation(out=warm_out[:], in_=warm_in[:], func=GELU)
-
         lists = [keep.tile([P, J // 16], U16, name="list%d" % i) for i in range(4)]
         pool_words = keep.tile([P, T], U32, name="pool_words", align_bytes=64)
         gain_sb = keep.tile([P, PACK], F32, name="gain_sb")
@@ -86,90 +76,113 @@ def tile_attend_nsa_compress_pl_kernel(tc, tok_words, tok_scales, w0, w1, w2, w3
         nc.sync.dma_start(out=gain_sb[:], in_=gain.rearrange("(p t) o -> p (t o)", t=PACK))
         wo_raw = load_raw("wo", wo, nc.sync)
 
+        nc.vector.memset(warm_in[:], 0.0)
+        nc.scalar.activation(out=warm_out[:], in_=warm_in[:], func=GELU)
         tok_s = []
         for i in range(4):
             s = keep.tile([P, J], U8, name="tok_s%d" % i, align_bytes=64)
             nc.vector.tensor_copy(out=s[:], in_=pool_scales[:].indirect(lists[i][:]))
             tok_s.append(s)
 
-        z = [[psum.tile([P, w], F32, name="z%d_%d" % (h, t), tag="bank%d" % (PACK * h + t)) for t in range(PACK)]
-             for h, w in enumerate(GELU_CHUNKS)]
+        z = [[psum.tile([P, HALF], F32, name="z%d_%d" % (h, t), tag="bank%d" % (PACK * h + t))
+              for t in range(PACK)] for h in range(2)]
         tok_w = []
-        for i in range(4):
-            g = keep.tile([P, J], U32, name="tok_w%d" % i, align_bytes=64)
+
+        def gather_words(i, tag):
+            g = keep.tile([P, J], U32, name="tok_w%d" % i, tag=tag, align_bytes=64)
             nc.vector.tensor_copy(out=g[:], in_=pool_words[:].indirect(lists[i][:]))
             tok_w.append(g)
+
+        for i in range(3):
+            gather_words(i, "tok_w%d" % i)
         width = F * PACK
-        bf01 = [keep.tile([P, width], BF16, name="w%d_bf" % i, align_bytes=64) for i in range(2)]
-        bf23 = keep.tile([P, 2 * width - OVERLAP], BF16, name="w23_bf", align_bytes=64)
-        groupeds = [bf01[0][:], bf01[1][:], bf23[:, width - OVERLAP:], bf23[:, :width]]
         for i in range(4):
-            grouped = groupeds[i]
+            codes, scales = mx_tiles("w%d" % i, F)
             if i < 3:
-                deal(nc.scalar.copy, grouped, raws[i], 0, P)
+                grouped = keep.tile([P, width], BF16, name="w%d_bf" % i, tag="w%d_bf" % i, align_bytes=64)
+                deal(nc.scalar.copy, grouped[:], raws[i], 0, PACK)
+                quantize(codes[:], scales[:], grouped[:])
             else:
-                deal(nc.scalar.copy, grouped, raws[i], 0, SPLIT3)
-                deal(nc.vector.tensor_copy, grouped, raws[i], SPLIT3, P)
-            codes, scales = quantize("w%d" % i, grouped, 1)
-            for h, (j0, w) in enumerate(spans(GELU_CHUNKS)):
+                low = keep.tile([P, width // 2], BF16, name="w3_low", align_bytes=64)
+                high = keep.tile([P, width // 2], BF16, name="w3_high", tag="w2_bf", align_bytes=64)
+                deal(nc.scalar.copy, low[:], raws[i], 0, 2)
+                deal(nc.vector.tensor_copy, high[:], raws[i], 2, PACK)
+                quantize(codes[:, :F // 2], scales[:, :F // 2], low[:])
+                quantize(codes[:, F // 2:], scales[:, F // 2:], high[:])
+            if i == 1:
+                gather_words(3, "w1_bf")
+            for h in range(2):
+                js = slice(h * HALF, (h + 1) * HALF)
                 for t in range(PACK):
                     cols = slice(t * P, (t + 1) * P)
                     nc.tensor.matmul_mx(out=z[h][t][:], lhsT=codes[:, cols].bitcast(FP8X4),
-                                        lhsT_scale=scales[:, cols],
-                                        rhs=tok_w[i][:, j0:j0 + w].bitcast(FP8X4),
-                                        rhs_scale=tok_s[i][:, j0:j0 + w], start=(i == 0), stop=(i == 3))
+                                        lhsT_scale=scales[:, cols], rhs=tok_w[i][:, js].bitcast(FP8X4),
+                                        rhs_scale=tok_s[i][:, js], start=(i == 0), stop=(i == 3))
 
         wo_bf = keep.tile([P, width], BF16, name="wo_bf", align_bytes=64)
-        deal(nc.vector.tensor_copy, wo_bf[:], wo_raw, SPLITO, P)
+        deal(nc.vector.tensor_copy, wo_bf[:], wo_raw, 0, PACK)
+        wo_codes, wo_scales = mx_tiles("wo", D)
+        quantize(wo_codes[:], wo_scales[:], wo_bf[:])
 
-        act = keep.tile([P, PACK, J], F32, name="act", align_bytes=64)
-        for c, (j0, w) in enumerate(spans(GELU_CHUNKS)):
+        acts = []
+        for h in range(2):
+            act = keep.tile([P, PACK, HALF], F32, name="act%d" % h, align_bytes=64)
             for t in range(PACK):
-                nc.scalar.activation(out=act[:, t, j0:j0 + w], in_=z[c][t][:], func=GELU)
-            if c == 0 and SPLITO > 0:
-                deal(nc.scalar.copy, wo_bf[:], wo_raw, 0, SPLITO)
-        wo_codes, wo_scales = quantize("wo", wo_bf[:], 1)
+                nc.scalar.activation(out=act[:, t, :], in_=z[h][t][:], func=GELU)
+            acts.append(act)
 
+        scaled = keep.tile([P, PACK, HALF], BF16, name="scaled", align_bytes=64)
+        for t in range(PACK):
+            nc.scalar.activation(out=scaled[:, t, :], in_=acts[1][:, t, :], func=COPY, scale=gain_sb[:, t:t + 1])
         hidden = []
-        for c, (j0, w) in enumerate(spans(CHUNKS)):
-            g_bf = keep.tile([P, w * PACK], BF16, name="g_bf%d" % c, align_bytes=64)
-            nc.vector.tensor_tensor(
-                out=g_bf[:].rearrange("p (c i t) -> p c t i", i=4, t=PACK),
-                in0=act[:, :, j0:j0 + w].rearrange("p t (c i) -> p c t i", i=4),
-                in1=gain_sb[:].unsqueeze(1).unsqueeze(3).to_broadcast([P, w // 4, PACK, 4]),
-                op=MULT)
-            g_codes = keep.tile([P, w], U32, name="g_codes%d" % c, align_bytes=64)
-            g_scales = keep.tile([P, w], U8, name="g_scales%d" % c, align_bytes=64)
-            nc.vector.quantize_mx(out=g_codes[:].bitcast(FP8X4), scales=g_scales[:], in_=g_bf[:])
+        starts = [sum(CHUNKS[:c]) for c in range(len(CHUNKS))]
+        for c, CH in enumerate(CHUNKS):
+            h, j0 = divmod(starts[c], HALF)
+            g_bf = keep.tile([P, CH * PACK], BF16, name="g_bf%d" % c, align_bytes=64)
+            if h == 0:
+                nc.vector.tensor_tensor(
+                    out=g_bf[:].rearrange("p (c i t) -> p c t i", i=4, t=PACK),
+                    in0=acts[h][:, :, j0:j0 + CH].rearrange("p t (c i) -> p c t i", i=4),
+                    in1=gain_sb[:].unsqueeze(1).unsqueeze(3).to_broadcast([P, CH // 4, PACK, 4]),
+                    op=MULT)
+            else:
+                nc.vector.tensor_copy(out=g_bf[:].rearrange("p (c i t) -> p c t i", i=4, t=PACK),
+                                      in_=scaled[:, :, j0:j0 + CH].rearrange("p t (c i) -> p c t i", i=4))
+            g_codes, g_scales = mx_tiles("g%d" % c, CH)
+            quantize(g_codes[:], g_scales[:], g_bf[:])
             hidden.append((g_codes, g_scales))
 
-        y = keep.tile([P, PACK, J], F32, name="y", align_bytes=64)
-        y_codes = keep.tile([P, J], U32, name="y_codes", align_bytes=64)
-        y_scales = keep.tile([P, J], U8, name="y_scales", align_bytes=64)
+        y_codes, y_scales = mx_tiles("y", J)
         out_rows = out_0.rearrange("(p t) j -> p t j", t=PACK)
         out_words = out_1[0].rearrange("p n t -> p (n t)").bitcast(I32)
-        y_ends = {a + n: a for a, n in spans(Y_STORES)}
-        word_ends = {a + n: a for a, n in spans(WORD_STORES)}
-        for c, (j0, w) in enumerate(spans(CHUNKS)):
-            g_codes, g_scales = hidden[c]
-            bank = psum.tile([P, PACK, w], F32, name="ybank%d" % c, tag="bank%d" % c)
-            for t in range(PACK):
-                cols = slice(t * P, (t + 1) * P)
-                nc.tensor.matmul_mx(out=bank[:, t, :], lhsT=wo_codes[:, cols].bitcast(FP8X4),
-                                    lhsT_scale=wo_scales[:, cols], rhs=g_codes[:].bitcast(FP8X4),
-                                    rhs_scale=g_scales[:], start=True, stop=True)
-            nc.scalar.copy(out=y[:, :, j0:j0 + w], in_=bank[:])
-            if j0 + w in y_ends:
-                a = y_ends[j0 + w]
-                nc.sync.dma_start(out=out_rows[:, :, a:j0 + w], in_=y[:, :, a:j0 + w])
-            y_bf = keep.tile([P, w * PACK], BF16, name="y_bf%d" % c, align_bytes=64)
-            nc.vector.tensor_copy(out=y_bf[:].rearrange("p (c i t) -> p c t i", i=4, t=PACK),
-                                  in_=y[:, :, j0:j0 + w].rearrange("p t (c i) -> p c t i", i=4))
-            nc.vector.quantize_mx(out=y_codes[:, j0:j0 + w].bitcast(FP8X4), scales=y_scales[:, j0:j0 + w],
-                                  in_=y_bf[:])
-            if j0 + w in word_ends:
-                a = word_ends[j0 + w]
-                nc.sync.dma_start(out=out_words[:, a:j0 + w], in_=y_codes[:, a:j0 + w].bitcast(I32))
+        stored = 0
+        for gi, group in enumerate(GROUPS):
+            j0, w = starts[group[0]], sum(CHUNKS[c] for c in group)
+            last = gi == len(GROUPS) - 1
+            y = keep.tile([P, PACK, w], F32, name="y%d" % gi, align_bytes=64)
+            y_bf = keep.tile([P, w * PACK], BF16, name="y_bf%d" % gi, align_bytes=64)
+            for u, c in enumerate(group):
+                g_codes, g_scales = hidden[c]
+                CH = CHUNKS[c]
+                a = starts[c] - j0
+                bank = psum.tile([P, PACK, CH], F32, name="ybank%d" % c, tag="bank%d" % c)
+                for t in range(PACK):
+                    cols = slice(t * P, (t + 1) * P)
+                    nc.tensor.matmul_mx(out=bank[:, t, :], lhsT=wo_codes[:, cols].bitcast(FP8X4),
+                                        lhsT_scale=wo_scales[:, cols], rhs=g_codes[:].bitcast(FP8X4),
+                                        rhs_scale=g_scales[:], start=True, stop=True)
+                if False:
+                    nc.vector.tensor_copy(out=y_bf[:].rearrange("p (j t) -> p j t", t=PACK),
+                                          in_=bank[:].rearrange("p t j -> p j t"))
+                nc.scalar.copy(out=y[:, :, a:a + CH], in_=bank[:])
+            nc.sync.dma_start(out=out_rows[:, :, j0:j0 + w], in_=y[:])
+            if True:
+                nc.vector.tensor_copy(out=y_bf[:].rearrange("p (c i t) -> p c t i", i=4, t=PACK),
+                                      in_=y[:].rearrange("p t (c i) -> p c t i", i=4))
+            quantize(y_codes[:, j0:j0 + w], y_scales[:, j0:j0 + w], y_bf[:])
+            if gi in WORD_STORES_AFTER:
+                nc.sync.dma_start(out=out_words[:, stored:j0 + w], in_=y_codes[:, stored:j0 + w].bitcast(I32))
+                stored = j0 + w
         for q in range(4):
             queue = nc.sync if q == 0 else nc.scalar
             queue.dma_start(out=out_2[0, 4 * q:4 * q + 4, :].bitcast(I32),

@@ -131,6 +131,10 @@ def tile_attend_nsa_compress_pl_kernel(tc, tok_words, tok_scales, w0, w1, w2, w3
                 nc.scalar.activation(out=act[:, t, :], in_=z[h][t][:], func=GELU)
             acts.append(act)
 
+        for t in range(PACK):
+            spare = psum.tile([P, J], F32, name="spare%d" % t, tag="bank%d" % (PACK + t))
+            nc.tensor.matmul_mx(out=spare[:], lhsT=codes[:, :P].bitcast(FP8X4), lhsT_scale=scales[:, :P],
+                                rhs=tok_w[3][:].bitcast(FP8X4), rhs_scale=tok_s[3][:], start=True, stop=True)
         scaled = keep.tile([P, PACK, HALF], BF16, name="scaled", align_bytes=64)
         for t in range(PACK):
             nc.scalar.activation(out=scaled[:, t, :], in_=acts[1][:, t, :], func=COPY, scale=gain_sb[:, t:t + 1])

@@ -16,28 +16,36 @@ MULT = mybir.AluOpType.mult
 P = 128
 PACK = 4
 K, T, J, F, D = 512, 2048, 512, 512, 512
-HALF = J // 2
-CHUNKS = [128, 128, 128, 128]
-GROUPS = [[0], [1], [2], [3]]
+CH = 128
+NCH = J // CH
+HALF = F // 2
+SCALED_ON_SCALAR = []
+ROUNDED_ON_SCALAR = [0, 3]
 WORD_STORES_AFTER = [2, 3]
+SPARE = 4
+FIRST = 128
+W3_SPLIT = 384
 FLOPS = 2 * (4 * K * F * J + F * D * J)
 
 
 def tile_attend_nsa_compress_pl_kernel(tc, tok_words, tok_scales, w0, w1, w2, w3, gain, wo,
-                                        offs, offs2, offs3, offs4, out_0, out_1, out_2):
+                                            offs, offs2, offs3, offs4, out_0, out_1, out_2):
     nc = tc.nc
     with ExitStack() as ctx:
         keep = ctx.enter_context(tc.tile_pool(name="keep", bufs=1))
         psum = ctx.enter_context(tc.psum_pool(name="psum", bufs=1))
 
-        def load_raw(name, w, queue):
-            raw = keep.tile([P, PACK, F], F32, name=name + "_raw", align_bytes=64)
-            queue.dma_start(out=raw[:], in_=w.rearrange("(p j) c -> p j c", j=PACK))
-            return raw
+        def load_piece(name, w, c0, c1):
+            raw = keep.tile([P, PACK, c1 - c0], F32, name="%s_raw%d" % (name, c0), align_bytes=64)
+            nc.sync.dma_start(out=raw[:], in_=w.rearrange("(p j) c -> p j c", j=PACK)[:, :, c0:c1])
+            return raw, c0, c1
 
-        def deal(copy, grouped, raw, t0, t1):
-            copy(out=grouped.rearrange("p (t m j) -> p m j t", t=t1 - t0, j=PACK),
-                 in_=raw[:].rearrange("p j (m t) -> p m j t", t=PACK)[:, :, :, t0:t1])
+        def deal(copy, grouped, piece, c0=None, c1=None):
+            raw, first, last = piece
+            c0 = first if c0 is None else c0
+            c1 = last if c1 is None else c1
+            copy(out=grouped[:].rearrange("p (t m j) -> p m j t", t=PACK, j=PACK)[:, c0 // PACK:c1 // PACK],
+                 in_=raw[:, :, c0 - first:c1 - first].rearrange("p j (m t) -> p m j t", t=PACK))
 
         def mx_tiles(name, n):
             codes = keep.tile([P, n], U32, name=name + "_codes", align_bytes=64)
@@ -47,6 +55,10 @@ def tile_attend_nsa_compress_pl_kernel(tc, tok_words, tok_scales, w0, w1, w2, w3
         def quantize(codes, scales, grouped):
             nc.vector.quantize_mx(out=codes.bitcast(FP8X4), scales=scales, in_=grouped)
 
+        def interleave(grouped, rows):
+            nc.vector.tensor_copy(out=grouped[:].rearrange("p (c i t) -> p c t i", i=4, t=PACK),
+                                  in_=rows[:].rearrange("p t (c i) -> p c t i", i=4))
+
         pool_scales = keep.tile([P, T], U8, name="pool_scales", align_bytes=64)
         warm_in = keep.tile([P, 1], F32, name="warm_in")
         warm_out = keep.tile([P, 1], F32, name="warm_out")
@@ -54,27 +66,25 @@ def tile_attend_nsa_compress_pl_kernel(tc, tok_words, tok_scales, w0, w1, w2, w3
         pool_words = keep.tile([P, T], U32, name="pool_words", align_bytes=64)
         gain_sb = keep.tile([P, PACK], F32, name="gain_sb")
 
-        def load_scales(q, queue):
-            rows = tok_scales[0, 4 * q:4 * q + 4, :].bitcast(I32)
-            queue.dma_start(out=pool_scales[32 * q:32 * q + 32, :].bitcast(I32),
-                            in_=rows.unsqueeze(0).to_broadcast([8, 4, T // 4]))
-
-        def load_words(queue):
-            queue.dma_start(out=pool_words[:].bitcast(I32),
-                            in_=tok_words[0].rearrange("p n t -> p (n t)").bitcast(I32))
-
+        nc.vector.memset(pool_scales[:].bitcast(I32), 0)
+        raws = {}
+        raws[0, 0] = load_piece("w0", w0, 0, FIRST)
         nc.sync.dma_start(lists[0][:], offs)
-        for q in range(4):
-            load_scales(q, nc.sync)
         nc.sync.dma_start(lists[1][:], offs2)
+        for q in (0, 2, 1, 3):
+            nc.sync.dma_start(out=pool_scales[32 * q:32 * q + 4, :].bitcast(I32),
+                              in_=tok_scales[0, 4 * q:4 * q + 4, :].bitcast(I32))
+        raws[0, 1] = load_piece("w0", w0, FIRST, F)
         nc.sync.dma_start(lists[2][:], offs3)
-        raws = [load_raw("w0", w0, nc.sync)]
         nc.sync.dma_start(lists[3][:], offs4)
-        load_words(nc.sync)
-        for i, w in ((1, w1), (2, w2), (3, w3)):
-            raws.append(load_raw("w%d" % i, w, nc.sync))
+        raws[1, 0] = load_piece("w1", w1, 0, HALF)
+        nc.sync.dma_start(out=pool_words[:].bitcast(I32),
+                          in_=tok_words[0].rearrange("p n t -> p (n t)").bitcast(I32))
+        raws[1, 1] = load_piece("w1", w1, HALF, F)
         nc.sync.dma_start(out=gain_sb[:], in_=gain.rearrange("(p t) o -> p (t o)", t=PACK))
-        wo_raw = load_raw("wo", wo, nc.sync)
+        for i, w in ((2, w2), (3, w3), (4, wo)):
+            for h in range(2):
+                raws[i, h] = load_piece("w%d" % i, w, h * HALF, (h + 1) * HALF)
 
         nc.vector.memset(warm_in[:], 0.0)
         nc.scalar.activation(out=warm_out[:], in_=warm_in[:], func=GELU)
@@ -84,8 +94,7 @@ def tile_attend_nsa_compress_pl_kernel(tc, tok_words, tok_scales, w0, w1, w2, w3
             nc.vector.tensor_copy(out=s[:], in_=pool_scales[:].indirect(lists[i][:]))
             tok_s.append(s)
 
-        z = [[psum.tile([P, HALF], F32, name="z%d_%d" % (h, t), tag="bank%d" % (PACK * h + t))
-              for t in range(PACK)] for h in range(2)]
+        z = [psum.tile([P, PACK, CH], F32, name="z%d" % c, tag="bank%d" % c) for c in range(NCH)]
         tok_w = []
 
         def gather_words(i, tag):
@@ -93,65 +102,79 @@ def tile_attend_nsa_compress_pl_kernel(tc, tok_words, tok_scales, w0, w1, w2, w3
             nc.vector.tensor_copy(out=g[:], in_=pool_words[:].indirect(lists[i][:]))
             tok_w.append(g)
 
-        for i in range(3):
-            gather_words(i, "tok_w%d" % i)
+        def first_layer(i, codes, scales, c, t):
+            cols = slice(t * P, (t + 1) * P)
+            js = slice(c * CH, (c + 1) * CH)
+            nc.tensor.matmul_mx(out=z[c][:, t, :], lhsT=codes[:, cols].bitcast(FP8X4),
+                                lhsT_scale=scales[:, cols], rhs=tok_w[i][:, js].bitcast(FP8X4),
+                                rhs_scale=tok_s[i][:, js], start=(i == 0 and t == 0),
+                                stop=(i == 3 and t == PACK - 1))
+
         width = F * PACK
+        for i in range(2):
+            gather_words(i, "tok_w%d" % i)
         for i in range(4):
             codes, scales = mx_tiles("w%d" % i, F)
+            grouped = keep.tile([P, width], BF16, name="w%d_bf" % i, tag="w%d_bf" % i, align_bytes=64)
+            deal(nc.scalar.copy, grouped, raws[i, 0])
             if i < 3:
-                grouped = keep.tile([P, width], BF16, name="w%d_bf" % i, tag="w%d_bf" % i, align_bytes=64)
-                deal(nc.scalar.copy, grouped[:], raws[i], 0, PACK)
+                deal(nc.scalar.copy, grouped, raws[i, 1])
+            else:
+                deal(nc.scalar.copy, grouped, raws[i, 1], HALF, W3_SPLIT)
+                deal(nc.vector.tensor_copy, grouped, raws[i, 1], W3_SPLIT, F)
+            if i < 3:
                 quantize(codes[:], scales[:], grouped[:])
             else:
-                low = keep.tile([P, width // 2], BF16, name="w3_low", align_bytes=64)
-                high = keep.tile([P, width // 2], BF16, name="w3_high", tag="w2_bf", align_bytes=64)
-                deal(nc.scalar.copy, low[:], raws[i], 0, 2)
-                deal(nc.vector.tensor_copy, high[:], raws[i], 2, PACK)
-                quantize(codes[:, :F // 2], scales[:, :F // 2], low[:])
-                quantize(codes[:, F // 2:], scales[:, F // 2:], high[:])
+                quantize(codes[:, :F // 2], scales[:, :F // 2], grouped[:, :width // 2])
+                quantize(codes[:, F // 2:], scales[:, F // 2:], grouped[:, width // 2:])
             if i == 1:
-                gather_words(3, "w1_bf")
-            for h in range(2):
-                js = slice(h * HALF, (h + 1) * HALF)
-                for t in range(PACK):
-                    cols = slice(t * P, (t + 1) * P)
-                    nc.tensor.matmul_mx(out=z[h][t][:], lhsT=codes[:, cols].bitcast(FP8X4),
-                                        lhsT_scale=scales[:, cols], rhs=tok_w[i][:, js].bitcast(FP8X4),
-                                        rhs_scale=tok_s[i][:, js], start=(i == 0), stop=(i == 3))
+                gather_words(2, "w1_bf")
+                gather_words(3, "tok_w3")
+            if i < 3:
+                for c in range(NCH):
+                    for t in range(PACK):
+                        first_layer(i, codes, scales, c, t)
+            else:
+                for cs in ((0, 1), (2, 3)):
+                    for ts in ((0, 1), (2, 3)):
+                        for c in cs:
+                            for t in ts:
+                                first_layer(i, codes, scales, c, t)
 
         wo_bf = keep.tile([P, width], BF16, name="wo_bf", align_bytes=64)
-        deal(nc.vector.tensor_copy, wo_bf[:], wo_raw, 0, PACK)
+        deal(nc.scalar.copy, wo_bf, raws[4, 0])
+        deal(nc.vector.tensor_copy, wo_bf, raws[4, 1])
         wo_codes, wo_scales = mx_tiles("wo", D)
         quantize(wo_codes[:], wo_scales[:], wo_bf[:])
 
+        ybanks = [psum.tile([P, PACK, CH], F32, name="ybank%d" % c, tag="bank%d" % (NCH + c)) for c in range(NCH)]
+        for u in range(SPARE):
+            nc.tensor.matmul_mx(out=ybanks[NCH - 1][:].rearrange("p t j -> p (t j)"),
+                                lhsT=codes[:, F - P:].bitcast(FP8X4), lhsT_scale=scales[:, F - P:],
+                                rhs=tok_w[3][:].bitcast(FP8X4), rhs_scale=tok_s[3][:], start=True, stop=True)
+
         acts = []
-        for h in range(2):
-            act = keep.tile([P, PACK, HALF], F32, name="act%d" % h, align_bytes=64)
-            for t in range(PACK):
-                nc.scalar.activation(out=act[:, t, :], in_=z[h][t][:], func=GELU)
+        for c in range(NCH):
+            if c in SCALED_ON_SCALAR:
+                act = keep.tile([P, PACK, CH], F32, name="act%d" % c, align_bytes=64)
+                nc.scalar.activation(out=act[:], in_=z[c][:], func=GELU)
+            else:
+                act = keep.tile([P, CH, PACK], F32, name="act%d" % c, align_bytes=64)
+                nc.scalar.activation(out=act[:], in_=z[c][:].rearrange("p t j -> p j t"), func=GELU)
             acts.append(act)
 
-        for t in range(PACK):
-            spare = psum.tile([P, J], F32, name="spare%d" % t, tag="bank%d" % (PACK + t))
-            nc.tensor.matmul_mx(out=spare[:], lhsT=codes[:, :P].bitcast(FP8X4), lhsT_scale=scales[:, :P],
-                                rhs=tok_w[3][:].bitcast(FP8X4), rhs_scale=tok_s[3][:], start=True, stop=True)
-        scaled = keep.tile([P, PACK, HALF], BF16, name="scaled", align_bytes=64)
-        for t in range(PACK):
-            nc.scalar.activation(out=scaled[:, t, :], in_=acts[1][:, t, :], func=COPY, scale=gain_sb[:, t:t + 1])
         hidden = []
-        starts = [sum(CHUNKS[:c]) for c in range(len(CHUNKS))]
-        for c, CH in enumerate(CHUNKS):
-            h, j0 = divmod(starts[c], HALF)
+        for c in range(NCH):
             g_bf = keep.tile([P, CH * PACK], BF16, name="g_bf%d" % c, align_bytes=64)
-            if h == 0:
-                nc.vector.tensor_tensor(
-                    out=g_bf[:].rearrange("p (c i t) -> p c t i", i=4, t=PACK),
-                    in0=acts[h][:, :, j0:j0 + CH].rearrange("p t (c i) -> p c t i", i=4),
-                    in1=gain_sb[:].unsqueeze(1).unsqueeze(3).to_broadcast([P, CH // 4, PACK, 4]),
-                    op=MULT)
+            if c in SCALED_ON_SCALAR:
+                scaled = keep.tile([P, PACK, CH], BF16, name="scaled%d" % c, align_bytes=64)
+                for t in range(PACK):
+                    nc.scalar.activation(out=scaled[:, t, :], in_=acts[c][:, t, :], func=COPY,
+                                         scale=gain_sb[:, t:t + 1])
+                interleave(g_bf, scaled)
             else:
-                nc.vector.tensor_copy(out=g_bf[:].rearrange("p (c i t) -> p c t i", i=4, t=PACK),
-                                      in_=scaled[:, :, j0:j0 + CH].rearrange("p t (c i) -> p c t i", i=4))
+                nc.vector.tensor_tensor(out=g_bf[:].rearrange("p (j t) -> p j t", t=PACK), in0=acts[c][:],
+                                        in1=gain_sb[:].unsqueeze(1).to_broadcast([P, CH, PACK]), op=MULT)
             g_codes, g_scales = mx_tiles("g%d" % c, CH)
             quantize(g_codes[:], g_scales[:], g_bf[:])
             hidden.append((g_codes, g_scales))
@@ -160,33 +183,28 @@ def tile_attend_nsa_compress_pl_kernel(tc, tok_words, tok_scales, w0, w1, w2, w3
         out_rows = out_0.rearrange("(p t) j -> p t j", t=PACK)
         out_words = out_1[0].rearrange("p n t -> p (n t)").bitcast(I32)
         stored = 0
-        for gi, group in enumerate(GROUPS):
-            j0, w = starts[group[0]], sum(CHUNKS[c] for c in group)
-            last = gi == len(GROUPS) - 1
-            y = keep.tile([P, PACK, w], F32, name="y%d" % gi, align_bytes=64)
-            y_bf = keep.tile([P, w * PACK], BF16, name="y_bf%d" % gi, align_bytes=64)
-            for u, c in enumerate(group):
-                g_codes, g_scales = hidden[c]
-                CH = CHUNKS[c]
-                a = starts[c] - j0
-                bank = psum.tile([P, PACK, CH], F32, name="ybank%d" % c, tag="bank%d" % c)
-                for t in range(PACK):
-                    cols = slice(t * P, (t + 1) * P)
-                    nc.tensor.matmul_mx(out=bank[:, t, :], lhsT=wo_codes[:, cols].bitcast(FP8X4),
-                                        lhsT_scale=wo_scales[:, cols], rhs=g_codes[:].bitcast(FP8X4),
-                                        rhs_scale=g_scales[:], start=True, stop=True)
-                if False:
-                    nc.vector.tensor_copy(out=y_bf[:].rearrange("p (j t) -> p j t", t=PACK),
-                                          in_=bank[:].rearrange("p t j -> p j t"))
-                nc.scalar.copy(out=y[:, :, a:a + CH], in_=bank[:])
-            nc.sync.dma_start(out=out_rows[:, :, j0:j0 + w], in_=y[:])
-            if True:
-                nc.vector.tensor_copy(out=y_bf[:].rearrange("p (c i t) -> p c t i", i=4, t=PACK),
-                                      in_=y[:].rearrange("p t (c i) -> p c t i", i=4))
-            quantize(y_codes[:, j0:j0 + w], y_scales[:, j0:j0 + w], y_bf[:])
-            if gi in WORD_STORES_AFTER:
-                nc.sync.dma_start(out=out_words[:, stored:j0 + w], in_=y_codes[:, stored:j0 + w].bitcast(I32))
-                stored = j0 + w
+        for c in range(NCH):
+            js = slice(c * CH, (c + 1) * CH)
+            y = keep.tile([P, PACK, CH], F32, name="y%d" % c, align_bytes=64)
+            y_bf = keep.tile([P, CH * PACK], BF16, name="y_bf%d" % c, align_bytes=64)
+            g_codes, g_scales = hidden[c]
+            for t in range(PACK):
+                cols = slice(t * P, (t + 1) * P)
+                nc.tensor.matmul_mx(out=ybanks[c][:, t, :], lhsT=wo_codes[:, cols].bitcast(FP8X4),
+                                    lhsT_scale=wo_scales[:, cols], rhs=g_codes[:].bitcast(FP8X4),
+                                    rhs_scale=g_scales[:], start=True, stop=True)
+            if c in ROUNDED_ON_SCALAR:
+                nc.scalar.copy(out=y_bf[:].rearrange("p (j t) -> p j t", t=PACK),
+                               in_=ybanks[c][:].rearrange("p t j -> p j t"))
+            nc.scalar.copy(out=y[:], in_=ybanks[c][:])
+            nc.sync.dma_start(out=out_rows[:, :, js], in_=y[:])
+            if c not in ROUNDED_ON_SCALAR:
+                interleave(y_bf, y)
+            quantize(y_codes[:, js], y_scales[:, js], y_bf[:])
+            if c in WORD_STORES_AFTER:
+                nc.sync.dma_start(out=out_words[:, stored:(c + 1) * CH],
+                                  in_=y_codes[:, stored:(c + 1) * CH].bitcast(I32))
+                stored = (c + 1) * CH
         for q in range(4):
             queue = nc.sync if q == 0 else nc.scalar
             queue.dma_start(out=out_2[0, 4 * q:4 * q + 4, :].bitcast(I32),

@@ -19,12 +19,13 @@ K, T, J, F, D = 512, 2048, 512, 512, 512
 CH = 128
 NCH = J // CH
 HALF = F // 2
-SCALED_ON_SCALAR = []
-ROUNDED_ON_SCALAR = [0, 3]
+SCALED_ON_SCALAR = [3]
+ROUNDED_ON_SCALAR = [3]
 WORD_STORES_AFTER = [2, 3]
 SPARE = 4
 FIRST = 128
 W3_SPLIT = 384
+WO_SPLIT = 352
 FLOPS = 2 * (4 * K * F * J + F * D * J)
 
 
@@ -36,7 +37,8 @@ def tile_attend_nsa_compress_pl_kernel(tc, tok_words, tok_scales, w0, w1, w2, w3
         psum = ctx.enter_context(tc.psum_pool(name="psum", bufs=1))
 
         def load_piece(name, w, c0, c1):
-            raw = keep.tile([P, PACK, c1 - c0], F32, name="%s_raw%d" % (name, c0), align_bytes=64)
+            raw = keep.tile([P, PACK, c1 - c0], F32, name="%s_raw%d" % (name, c0), tag="%s_raw%d" % (name, c0),
+                            align_bytes=64)
             nc.sync.dma_start(out=raw[:], in_=w.rearrange("(p j) c -> p j c", j=PACK)[:, :, c0:c1])
             return raw, c0, c1
 
@@ -143,7 +145,8 @@ def tile_attend_nsa_compress_pl_kernel(tc, tok_words, tok_scales, w0, w1, w2, w3
 
         wo_bf = keep.tile([P, width], BF16, name="wo_bf", align_bytes=64)
         deal(nc.scalar.copy, wo_bf, raws[4, 0])
-        deal(nc.vector.tensor_copy, wo_bf, raws[4, 1])
+        deal(nc.scalar.copy, wo_bf, raws[4, 1], HALF, WO_SPLIT)
+        deal(nc.vector.tensor_copy, wo_bf, raws[4, 1], WO_SPLIT, D)
         wo_codes, wo_scales = mx_tiles("wo", D)
         quantize(wo_codes[:], wo_scales[:], wo_bf[:])
 
@@ -154,13 +157,15 @@ def tile_attend_nsa_compress_pl_kernel(tc, tok_words, tok_scales, w0, w1, w2, w3
                                 rhs=tok_w[3][:].bitcast(FP8X4), rhs_scale=tok_s[3][:], start=True, stop=True)
 
         acts = []
+        act_all = keep.tile([P, J * PACK], F32, name="act_all", tag="w4_raw%d" % HALF, align_bytes=64)
         for c in range(NCH):
+            act = act_all[:, c * CH * PACK:(c + 1) * CH * PACK]
             if c in SCALED_ON_SCALAR:
-                act = keep.tile([P, PACK, CH], F32, name="act%d" % c, align_bytes=64)
-                nc.scalar.activation(out=act[:], in_=z[c][:], func=GELU)
+                act = act.rearrange("p (t j) -> p t j", t=PACK)
+                nc.scalar.activation(out=act, in_=z[c][:], func=GELU)
             else:
-                act = keep.tile([P, CH, PACK], F32, name="act%d" % c, align_bytes=64)
-                nc.scalar.activation(out=act[:], in_=z[c][:].rearrange("p t j -> p j t"), func=GELU)
+                act = act.rearrange("p (j t) -> p j t", t=PACK)
+                nc.scalar.activation(out=act, in_=z[c][:].rearrange("p t j -> p j t"), func=GELU)
             acts.append(act)
 
         hidden = []
@@ -173,7 +178,7 @@ def tile_attend_nsa_compress_pl_kernel(tc, tok_words, tok_scales, w0, w1, w2, w3
                                          scale=gain_sb[:, t:t + 1])
                 interleave(g_bf, scaled)
             else:
-                nc.vector.tensor_tensor(out=g_bf[:].rearrange("p (j t) -> p j t", t=PACK), in0=acts[c][:],
+                nc.vector.tensor_tensor(out=g_bf[:].rearrange("p (j t) -> p j t", t=PACK), in0=acts[c],
                                         in1=gain_sb[:].unsqueeze(1).to_broadcast([P, CH, PACK]), op=MULT)
             g_codes, g_scales = mx_tiles("g%d" % c, CH)
             quantize(g_codes[:], g_scales[:], g_bf[:])

@@ -19,9 +19,7 @@ K, T, J, F, D = 512, 2048, 512, 512, 512
 CH = 128
 NCH = J // CH
 HALF = F // 2
-SCALED_ON_SCALAR = [3]
-ROUNDED_ON_SCALAR = [3]
-WORD_STORES_AFTER = [2, 3]
+SCALED_ON_SCALAR = []
 SPARE = 4
 FIRST = 128
 W3_SPLIT = 384
@@ -58,8 +56,8 @@ def tile_attend_nsa_compress_pl_kernel(tc, tok_words, tok_scales, w0, w1, w2, w3
             nc.vector.quantize_mx(out=codes.bitcast(FP8X4), scales=scales, in_=grouped)
 
         def interleave(grouped, rows):
-            nc.vector.tensor_copy(out=grouped[:].rearrange("p (c i t) -> p c t i", i=4, t=PACK),
-                                  in_=rows[:].rearrange("p t (c i) -> p c t i", i=4))
+            nc.vector.tensor_copy(out=grouped.rearrange("p (c i t) -> p c t i", i=4, t=PACK),
+                                  in_=rows.rearrange("p t (c i) -> p c t i", i=4))
 
         pool_scales = keep.tile([P, T], U8, name="pool_scales", align_bytes=64)
         warm_in = keep.tile([P, 1], F32, name="warm_in")
@@ -176,7 +174,7 @@ def tile_attend_nsa_compress_pl_kernel(tc, tok_words, tok_scales, w0, w1, w2, w3
                 for t in range(PACK):
                     nc.scalar.activation(out=scaled[:, t, :], in_=acts[c][:, t, :], func=COPY,
                                          scale=gain_sb[:, t:t + 1])
-                interleave(g_bf, scaled)
+                interleave(g_bf[:], scaled[:])
             else:
                 nc.vector.tensor_tensor(out=g_bf[:].rearrange("p (j t) -> p j t", t=PACK), in0=acts[c],
                                         in1=gain_sb[:].unsqueeze(1).to_broadcast([P, CH, PACK]), op=MULT)
@@ -187,29 +185,28 @@ def tile_attend_nsa_compress_pl_kernel(tc, tok_words, tok_scales, w0, w1, w2, w3
         y_codes, y_scales = mx_tiles("y", J)
         out_rows = out_0.rearrange("(p t) j -> p t j", t=PACK)
         out_words = out_1[0].rearrange("p n t -> p (n t)").bitcast(I32)
-        stored = 0
-        for c in range(NCH):
-            js = slice(c * CH, (c + 1) * CH)
-            y = keep.tile([P, PACK, CH], F32, name="y%d" % c, align_bytes=64)
-            y_bf = keep.tile([P, CH * PACK], BF16, name="y_bf%d" % c, align_bytes=64)
-            g_codes, g_scales = hidden[c]
-            for t in range(PACK):
-                cols = slice(t * P, (t + 1) * P)
-                nc.tensor.matmul_mx(out=ybanks[c][:, t, :], lhsT=wo_codes[:, cols].bitcast(FP8X4),
-                                    lhsT_scale=wo_scales[:, cols], rhs=g_codes[:].bitcast(FP8X4),
-                                    rhs_scale=g_scales[:], start=True, stop=True)
-            if c in ROUNDED_ON_SCALAR:
-                nc.scalar.copy(out=y_bf[:].rearrange("p (j t) -> p j t", t=PACK),
-                               in_=ybanks[c][:].rearrange("p t j -> p j t"))
-            nc.scalar.copy(out=y[:], in_=ybanks[c][:])
-            nc.sync.dma_start(out=out_rows[:, :, js], in_=y[:])
-            if c not in ROUNDED_ON_SCALAR:
-                interleave(y_bf, y)
+        pair = 2 * CH
+        for u in range(NCH // 2):
+            y = keep.tile([P, PACK, pair], F32, name="y%d" % u, align_bytes=64)
+            y_bf = keep.tile([P, pair * PACK], BF16, name="y_bf%d" % u, align_bytes=64)
+            for e in range(2):
+                c = 2 * u + e
+                g_codes, g_scales = hidden[c]
+                for t in range(PACK):
+                    cols = slice(t * P, (t + 1) * P)
+                    nc.tensor.matmul_mx(out=ybanks[c][:, t, :], lhsT=wo_codes[:, cols].bitcast(FP8X4),
+                                        lhsT_scale=wo_scales[:, cols], rhs=g_codes[:].bitcast(FP8X4),
+                                        rhs_scale=g_scales[:], start=True, stop=True)
+                if c == NCH - 1:
+                    nc.scalar.copy(out=y_bf[:, CH * PACK:].rearrange("p (j t) -> p j t", t=PACK),
+                                   in_=ybanks[c][:].rearrange("p t j -> p j t"))
+                nc.scalar.copy(out=y[:, :, e * CH:(e + 1) * CH], in_=ybanks[c][:])
+                nc.sync.dma_start(out=out_rows[:, :, c * CH:(c + 1) * CH], in_=y[:, :, e * CH:(e + 1) * CH])
+                if c < NCH - 1:
+                    interleave(y_bf[:, e * CH * PACK:(e + 1) * CH * PACK], y[:, :, e * CH:(e + 1) * CH])
+            js = slice(u * pair, (u + 1) * pair)
             quantize(y_codes[:, js], y_scales[:, js], y_bf[:])
-            if c in WORD_STORES_AFTER:
-                nc.sync.dma_start(out=out_words[:, stored:(c + 1) * CH],
-                                  in_=y_codes[:, stored:(c + 1) * CH].bitcast(I32))
-                stored = (c + 1) * CH
+            nc.sync.dma_start(out=out_words[:, js], in_=y_codes[:, js].bitcast(I32))
         for q in range(4):
             queue = nc.sync if q == 0 else nc.scalar
             queue.dma_start(out=out_2[0, 4 * q:4 * q + 4, :].bitcast(I32),

@@ -19,11 +19,11 @@ K, T, J, F, D = 512, 2048, 512, 512, 512
 CH = 128
 NCH = J // CH
 HALF = F // 2
-SCALED_ON_SCALAR = []
+SCALED_ON_SCALAR = [3]
 SPARE = 4
 FIRST = 128
-W3_SPLIT = 384
-WO_SPLIT = 352
+W3_SPLIT = 336
+WO_SPLIT = 160
 FLOPS = 2 * (4 * K * F * J + F * D * J)
 
 
@@ -81,10 +81,11 @@ def tile_attend_nsa_compress_pl_kernel(tc, tok_words, tok_scales, w0, w1, w2, w3
         nc.sync.dma_start(out=pool_words[:].bitcast(I32),
                           in_=tok_words[0].rearrange("p n t -> p (n t)").bitcast(I32))
         raws[1, 1] = load_piece("w1", w1, HALF, F)
-        nc.sync.dma_start(out=gain_sb[:], in_=gain.rearrange("(p t) o -> p (t o)", t=PACK))
-        for i, w in ((2, w2), (3, w3), (4, wo)):
+        for i, w in ((2, w2), (3, w3)):
             for h in range(2):
                 raws[i, h] = load_piece("w%d" % i, w, h * HALF, (h + 1) * HALF)
+        wo_raws = [load_piece("wo", wo, c0, c1) for c0, c1 in ((0, HALF), (HALF, D - P), (D - P, D))]
+        nc.sync.dma_start(out=gain_sb[:], in_=gain.rearrange("(p t) o -> p (t o)", t=PACK))
 
         nc.vector.memset(warm_in[:], 0.0)
         nc.scalar.activation(out=warm_out[:], in_=warm_in[:], func=GELU)
@@ -111,7 +112,7 @@ def tile_attend_nsa_compress_pl_kernel(tc, tok_words, tok_scales, w0, w1, w2, w3
                                 stop=(i == 3 and t == PACK - 1))
 
         width = F * PACK
-        for i in range(2):
+        for i in range(3):
             gather_words(i, "tok_w%d" % i)
         for i in range(4):
             codes, scales = mx_tiles("w%d" % i, F)
@@ -128,8 +129,7 @@ def tile_attend_nsa_compress_pl_kernel(tc, tok_words, tok_scales, w0, w1, w2, w3
                 quantize(codes[:, :F // 2], scales[:, :F // 2], grouped[:, :width // 2])
                 quantize(codes[:, F // 2:], scales[:, F // 2:], grouped[:, width // 2:])
             if i == 1:
-                gather_words(2, "w1_bf")
-                gather_words(3, "tok_w3")
+                gather_words(3, "w1_bf")
             if i < 3:
                 for c in range(NCH):
                     for t in range(PACK):
@@ -142,11 +142,20 @@ def tile_attend_nsa_compress_pl_kernel(tc, tok_words, tok_scales, w0, w1, w2, w3
                                 first_layer(i, codes, scales, c, t)
 
         wo_bf = keep.tile([P, width], BF16, name="wo_bf", align_bytes=64)
-        deal(nc.scalar.copy, wo_bf, raws[4, 0])
-        deal(nc.scalar.copy, wo_bf, raws[4, 1], HALF, WO_SPLIT)
-        deal(nc.vector.tensor_copy, wo_bf, raws[4, 1], WO_SPLIT, D)
+        deal(nc.scalar.copy, wo_bf, wo_raws[0], 0, WO_SPLIT)
+        deal(nc.vector.tensor_copy, wo_bf, wo_raws[0], WO_SPLIT, HALF)
         wo_codes, wo_scales = mx_tiles("wo", D)
-        quantize(wo_codes[:], wo_scales[:], wo_bf[:])
+
+        def quantize_wo_half(h):
+            for t in range(PACK):
+                c0 = t * P + h * P // 2
+                quantize(wo_codes[:, c0:c0 + P // 2], wo_scales[:, c0:c0 + P // 2],
+                         wo_bf[:, c0 * PACK:(c0 + P // 2) * PACK])
+
+        quantize_wo_half(0)
+        deal(nc.vector.tensor_copy, wo_bf, wo_raws[1])
+        deal(nc.vector.tensor_copy, wo_bf, wo_raws[2])
+        quantize_wo_half(1)
 
         ybanks = [psum.tile([P, PACK, CH], F32, name="ybank%d" % c, tag="bank%d" % (NCH + c)) for c in range(NCH)]
         for u in range(SPARE):
@@ -155,7 +164,7 @@ def tile_attend_nsa_compress_pl_kernel(tc, tok_words, tok_scales, w0, w1, w2, w3
                                 rhs=tok_w[3][:].bitcast(FP8X4), rhs_scale=tok_s[3][:], start=True, stop=True)
 
         acts = []
-        act_all = keep.tile([P, J * PACK], F32, name="act_all", tag="w4_raw%d" % HALF, align_bytes=64)
+        act_all = keep.tile([P, J * PACK], F32, name="act_all", align_bytes=64)
         for c in range(NCH):
             act = act_all[:, c * CH * PACK:(c + 1) * CH * PACK]
             if c in SCALED_ON_SCALAR:

@@ -19,11 +19,10 @@ K, T, J, F, D = 512, 2048, 512, 512, 512
 CH = 128
 NCH = J // CH
 HALF = F // 2
-SCALED_ON_SCALAR = [3]
+SCALED_ON_SCALAR = []
 SPARE = 4
 FIRST = 128
-W3_SPLIT = 336
-WO_SPLIT = 160
+W3_SPLIT = 288
 FLOPS = 2 * (4 * K * F * J + F * D * J)
 
 
@@ -129,7 +128,7 @@ def tile_attend_nsa_compress_pl_kernel(tc, tok_words, tok_scales, w0, w1, w2, w3
                 quantize(codes[:, :F // 2], scales[:, :F // 2], grouped[:, :width // 2])
                 quantize(codes[:, F // 2:], scales[:, F // 2:], grouped[:, width // 2:])
             if i == 1:
-                gather_words(3, "w1_bf")
+                gather_words(3, "w1_raw%d" % HALF)
             if i < 3:
                 for c in range(NCH):
                     for t in range(PACK):
@@ -142,8 +141,7 @@ def tile_attend_nsa_compress_pl_kernel(tc, tok_words, tok_scales, w0, w1, w2, w3
                                 first_layer(i, codes, scales, c, t)
 
         wo_bf = keep.tile([P, width], BF16, name="wo_bf", align_bytes=64)
-        deal(nc.scalar.copy, wo_bf, wo_raws[0], 0, WO_SPLIT)
-        deal(nc.vector.tensor_copy, wo_bf, wo_raws[0], WO_SPLIT, HALF)
+        deal(nc.scalar.copy, wo_bf, wo_raws[0])
         wo_codes, wo_scales = mx_tiles("wo", D)
 
         def quantize_wo_half(h):

@@ -21,8 +21,8 @@ NCH = J // CH
 HALF = F // 2
 SCALED_ON_SCALAR = []
 SPARE = 4
-FIRST = 128
-W3_SPLIT = 288
+FIRST = 64
+W3_SPLIT = 336
 FLOPS = 2 * (4 * K * F * J + F * D * J)
 
 
@@ -67,23 +67,21 @@ def tile_attend_nsa_compress_pl_kernel(tc, tok_words, tok_scales, w0, w1, w2, w3
 
         nc.vector.memset(pool_scales[:].bitcast(I32), 0)
         raws = {}
-        raws[0, 0] = load_piece("w0", w0, 0, FIRST)
+        wo_raws = [load_piece("wo", wo, 0, FIRST)]
         nc.sync.dma_start(lists[0][:], offs)
         nc.sync.dma_start(lists[1][:], offs2)
         for q in (0, 2, 1, 3):
             nc.sync.dma_start(out=pool_scales[32 * q:32 * q + 4, :].bitcast(I32),
                               in_=tok_scales[0, 4 * q:4 * q + 4, :].bitcast(I32))
-        raws[0, 1] = load_piece("w0", w0, FIRST, F)
+        raws[0] = [load_piece("w0", w0, 0, F)]
         nc.sync.dma_start(lists[2][:], offs3)
         nc.sync.dma_start(lists[3][:], offs4)
-        raws[1, 0] = load_piece("w1", w1, 0, HALF)
         nc.sync.dma_start(out=pool_words[:].bitcast(I32),
                           in_=tok_words[0].rearrange("p n t -> p (n t)").bitcast(I32))
-        raws[1, 1] = load_piece("w1", w1, HALF, F)
-        for i, w in ((2, w2), (3, w3)):
-            for h in range(2):
-                raws[i, h] = load_piece("w%d" % i, w, h * HALF, (h + 1) * HALF)
-        wo_raws = [load_piece("wo", wo, c0, c1) for c0, c1 in ((0, HALF), (HALF, D - P), (D - P, D))]
+        raws[1] = [load_piece("w1", w1, 0, F)]
+        raws[2] = [load_piece("w2", w2, 0, F)]
+        raws[3] = [load_piece("w3", w3, 0, HALF), load_piece("w3", w3, HALF, F)]
+        wo_raws.extend([load_piece("wo", wo, FIRST, D - P), load_piece("wo", wo, D - P, D)])
         nc.sync.dma_start(out=gain_sb[:], in_=gain.rearrange("(p t) o -> p (t o)", t=PACK))
 
         nc.vector.memset(warm_in[:], 0.0)
@@ -116,19 +114,17 @@ def tile_attend_nsa_compress_pl_kernel(tc, tok_words, tok_scales, w0, w1, w2, w3
         for i in range(4):
             codes, scales = mx_tiles("w%d" % i, F)
             grouped = keep.tile([P, width], BF16, name="w%d_bf" % i, tag="w%d_bf" % i, align_bytes=64)
-            deal(nc.scalar.copy, grouped, raws[i, 0])
-            if i < 3:
-                deal(nc.scalar.copy, grouped, raws[i, 1])
-            else:
-                deal(nc.scalar.copy, grouped, raws[i, 1], HALF, W3_SPLIT)
-                deal(nc.vector.tensor_copy, grouped, raws[i, 1], W3_SPLIT, F)
+            deal(nc.scalar.copy, grouped, raws[i][0])
+            if i == 3:
+                deal(nc.scalar.copy, grouped, raws[i][1], HALF, W3_SPLIT)
+                deal(nc.vector.tensor_copy, grouped, raws[i][1], W3_SPLIT, F)
             if i < 3:
                 quantize(codes[:], scales[:], grouped[:])
             else:
                 quantize(codes[:, :F // 2], scales[:, :F // 2], grouped[:, :width // 2])
                 quantize(codes[:, F // 2:], scales[:, F // 2:], grouped[:, width // 2:])
             if i == 1:
-                gather_words(3, "w1_raw%d" % HALF)
+                gather_words(3, "w1_raw0")
             if i < 3:
                 for c in range(NCH):
                     for t in range(PACK):
@@ -142,6 +138,7 @@ def tile_attend_nsa_compress_pl_kernel(tc, tok_words, tok_scales, w0, w1, w2, w3
 
         wo_bf = keep.tile([P, width], BF16, name="wo_bf", align_bytes=64)
         deal(nc.scalar.copy, wo_bf, wo_raws[0])
+        deal(nc.scalar.copy, wo_bf, wo_raws[1], FIRST, HALF)
         wo_codes, wo_scales = mx_tiles("wo", D)
 
         def quantize_wo_half(h):
@@ -151,7 +148,7 @@ def tile_attend_nsa_compress_pl_kernel(tc, tok_words, tok_scales, w0, w1, w2, w3
                          wo_bf[:, c0 * PACK:(c0 + P // 2) * PACK])
 
         quantize_wo_half(0)
-        deal(nc.vector.tensor_copy, wo_bf, wo_raws[1])
+        deal(nc.vector.tensor_copy, wo_bf, wo_raws[1], HALF, D - P)
         deal(nc.vector.tensor_copy, wo_bf, wo_raws[2])
         quantize_wo_half(1)
 

@@ -10,7 +10,6 @@ U16 = mybir.dt.uint16
 U8 = mybir.dt.uint8
 FP8X4 = mybir.dt.float8_e4m3fn_x4
 GELU = mybir.ActivationFunctionType.Gelu_apprx_tanh
-COPY = mybir.ActivationFunctionType.Copy
 MULT = mybir.AluOpType.mult
 
 P = 128
@@ -19,8 +18,7 @@ K, T, J, F, D = 512, 2048, 512, 512, 512
 CH = 128
 NCH = J // CH
 HALF = F // 2
-SCALED_ON_SCALAR = []
-SPARE = 4
+SPARE = 2
 FIRST = 64
 W3_SPLIT = 336
 FLOPS = 2 * (4 * K * F * J + F * D * J)
@@ -156,32 +154,21 @@ def tile_attend_nsa_compress_pl_kernel(tc, tok_words, tok_scales, w0, w1, w2, w3
         for u in range(SPARE):
             nc.tensor.matmul_mx(out=ybanks[NCH - 1][:].rearrange("p t j -> p (t j)"),
                                 lhsT=codes[:, F - P:].bitcast(FP8X4), lhsT_scale=scales[:, F - P:],
-                                rhs=tok_w[3][:].bitcast(FP8X4), rhs_scale=tok_s[3][:], start=True, stop=True)
+                                rhs=codes[:].bitcast(FP8X4), rhs_scale=scales[:], start=True, stop=True)
 
         acts = []
         act_all = keep.tile([P, J * PACK], F32, name="act_all", align_bytes=64)
         for c in range(NCH):
             act = act_all[:, c * CH * PACK:(c + 1) * CH * PACK]
-            if c in SCALED_ON_SCALAR:
-                act = act.rearrange("p (t j) -> p t j", t=PACK)
-                nc.scalar.activation(out=act, in_=z[c][:], func=GELU)
-            else:
-                act = act.rearrange("p (j t) -> p j t", t=PACK)
-                nc.scalar.activation(out=act, in_=z[c][:].rearrange("p t j -> p j t"), func=GELU)
+            act = act.rearrange("p (j t) -> p j t", t=PACK)
+            nc.scalar.activation(out=act, in_=z[c][:].rearrange("p t j -> p j t"), func=GELU)
             acts.append(act)
 
         hidden = []
         for c in range(NCH):
             g_bf = keep.tile([P, CH * PACK], BF16, name="g_bf%d" % c, align_bytes=64)
-            if c in SCALED_ON_SCALAR:
-                scaled = keep.tile([P, PACK, CH], BF16, name="scaled%d" % c, align_bytes=64)
-                for t in range(PACK):
-                    nc.scalar.activation(out=scaled[:, t, :], in_=acts[c][:, t, :], func=COPY,
-                                         scale=gain_sb[:, t:t + 1])
-                interleave(g_bf[:], scaled[:])
-            else:
-                nc.vector.tensor_tensor(out=g_bf[:].rearrange("p (j t) -> p j t", t=PACK), in0=acts[c],
-                                        in1=gain_sb[:].unsqueeze(1).to_broadcast([P, CH, PACK]), op=MULT)
+            nc.vector.tensor_tensor(out=g_bf[:].rearrange("p (j t) -> p j t", t=PACK), in0=acts[c],
+                                    in1=gain_sb[:].unsqueeze(1).to_broadcast([P, CH, PACK]), op=MULT)
             g_codes, g_scales = mx_tiles("g%d" % c, CH)
             quantize(g_codes[:], g_scales[:], g_bf[:])
             hidden.append((g_codes, g_scales))

@@ -188,15 +188,20 @@ def tile_attend_nsa_compress_pl_kernel(tc, tok_words, tok_scales, w0, w1, w2, w3
                     nc.tensor.matmul_mx(out=ybanks[c][:, t, :], lhsT=wo_codes[:, cols].bitcast(FP8X4),
                                         lhsT_scale=wo_scales[:, cols], rhs=g_codes[:].bitcast(FP8X4),
                                         rhs_scale=g_scales[:], start=True, stop=True)
+                nc.scalar.copy(out=y[:, :, e * CH:(e + 1) * CH], in_=ybanks[c][:])
+                nc.sync.dma_start(out=out_rows[:, :, c * CH:(c + 1) * CH], in_=y[:, :, e * CH:(e + 1) * CH])
                 if c == NCH - 1:
                     nc.scalar.copy(out=y_bf[:, CH * PACK:].rearrange("p (j t) -> p j t", t=PACK),
                                    in_=ybanks[c][:].rearrange("p t j -> p j t"))
-                nc.scalar.copy(out=y[:, :, e * CH:(e + 1) * CH], in_=ybanks[c][:])
-                nc.sync.dma_start(out=out_rows[:, :, c * CH:(c + 1) * CH], in_=y[:, :, e * CH:(e + 1) * CH])
                 if c < NCH - 1:
                     interleave(y_bf[:, e * CH * PACK:(e + 1) * CH * PACK], y[:, :, e * CH:(e + 1) * CH])
             js = slice(u * pair, (u + 1) * pair)
-            quantize(y_codes[:, js], y_scales[:, js], y_bf[:])
+            if u == 0:
+                quantize(y_codes[:, js], y_scales[:, js], y_bf[:])
+            else:
+                for e in range(2):
+                    cj = slice(u * pair + e * CH, u * pair + (e + 1) * CH)
+                    quantize(y_codes[:, cj], y_scales[:, cj], y_bf[:, e * CH * PACK:(e + 1) * CH * PACK])
             nc.sync.dma_start(out=out_words[:, js], in_=y_codes[:, js].bitcast(I32))
         for q in range(4):
             queue = nc.sync if q == 0 else nc.scalar

@@ -19,8 +19,7 @@ CH = 128
 NCH = J // CH
 HALF = F // 2
 SPARE = 2
-FIRST = 64
-W3_SPLIT = 336
+W3_SPLIT = 376
 FLOPS = 2 * (4 * K * F * J + F * D * J)
 
 
@@ -65,13 +64,16 @@ def tile_attend_nsa_compress_pl_kernel(tc, tok_words, tok_scales, w0, w1, w2, w3
 
         nc.vector.memset(pool_scales[:].bitcast(I32), 0)
         raws = {}
-        wo_raws = [load_piece("wo", wo, 0, FIRST)]
+        w0_raw = keep.tile([P, PACK, F], F32, name="w0_raw", align_bytes=64)
+        w0_rows = w0.rearrange("(p j) c -> p j c", j=PACK)
+        nc.sync.dma_start(out=w0_raw[:, 0, :], in_=w0_rows[:, 0, :])
         nc.sync.dma_start(lists[0][:], offs)
         nc.sync.dma_start(lists[1][:], offs2)
         for q in (0, 2, 1, 3):
             nc.sync.dma_start(out=pool_scales[32 * q:32 * q + 4, :].bitcast(I32),
                               in_=tok_scales[0, 4 * q:4 * q + 4, :].bitcast(I32))
-        raws[0] = [load_piece("w0", w0, 0, F)]
+        nc.sync.dma_start(out=w0_raw[:, 1:, :], in_=w0_rows[:, 1:, :])
+        raws[0] = [(w0_raw, 0, F)]
         nc.sync.dma_start(lists[2][:], offs3)
         nc.sync.dma_start(lists[3][:], offs4)
         nc.sync.dma_start(out=pool_words[:].bitcast(I32),
@@ -79,7 +81,7 @@ def tile_attend_nsa_compress_pl_kernel(tc, tok_words, tok_scales, w0, w1, w2, w3
         raws[1] = [load_piece("w1", w1, 0, F)]
         raws[2] = [load_piece("w2", w2, 0, F)]
         raws[3] = [load_piece("w3", w3, 0, HALF), load_piece("w3", w3, HALF, F)]
-        wo_raws.extend([load_piece("wo", wo, FIRST, D - P), load_piece("wo", wo, D - P, D)])
+        wo_raws = [load_piece("wo", wo, 0, D - P), load_piece("wo", wo, D - P, D)]
         nc.sync.dma_start(out=gain_sb[:], in_=gain.rearrange("(p t) o -> p (t o)", t=PACK))
 
         nc.vector.memset(warm_in[:], 0.0)
@@ -135,8 +137,7 @@ def tile_attend_nsa_compress_pl_kernel(tc, tok_words, tok_scales, w0, w1, w2, w3
                                 first_layer(i, codes, scales, c, t)
 
         wo_bf = keep.tile([P, width], BF16, name="wo_bf", align_bytes=64)
-        deal(nc.scalar.copy, wo_bf, wo_raws[0])
-        deal(nc.scalar.copy, wo_bf, wo_raws[1], FIRST, HALF)
+        deal(nc.scalar.copy, wo_bf, wo_raws[0], 0, HALF)
         wo_codes, wo_scales = mx_tiles("wo", D)
 
         def quantize_wo_half(h):
@@ -145,9 +146,9 @@ def tile_attend_nsa_compress_pl_kernel(tc, tok_words, tok_scales, w0, w1, w2, w3
                 quantize(wo_codes[:, c0:c0 + P // 2], wo_scales[:, c0:c0 + P // 2],
                          wo_bf[:, c0 * PACK:(c0 + P // 2) * PACK])
 
+        deal(nc.vector.tensor_copy, wo_bf, wo_raws[0], HALF, D - P)
+        deal(nc.vector.tensor_copy, wo_bf, wo_raws[1])
         quantize_wo_half(0)
-        deal(nc.vector.tensor_copy, wo_bf, wo_raws[1], HALF, D - P)
-        deal(nc.vector.tensor_copy, wo_bf, wo_raws[2])
         quantize_wo_half(1)
 
         ybanks = [psum.tile([P, PACK, CH], F32, name="ybank%d" % c, tag="bank%d" % (NCH + c)) for c in range(NCH)]

@@ -19,7 +19,7 @@ CH = 128
 NCH = J // CH
 HALF = F // 2
 SPARE = 2
-W3_SPLIT = 376
+W3_SPLIT = 328
 FLOPS = 2 * (4 * K * F * J + F * D * J)
 
 

from contextlib import ExitStack

import concourse.mybir as mybir

F32 = mybir.dt.float32
BF16 = mybir.dt.bfloat16
I32 = mybir.dt.int32
U32 = mybir.dt.uint32
U16 = mybir.dt.uint16
U8 = mybir.dt.uint8
FP8X4 = mybir.dt.float8_e4m3fn_x4
GELU = mybir.ActivationFunctionType.Gelu_apprx_tanh
MULT = mybir.AluOpType.mult

P = 128
PACK = 4
K, T, J, F, D = 512, 2048, 512, 512, 512
CH = 128
NCH = J // CH
HALF = F // 2
SPARE = 2
W3_SPLIT = 328
FLOPS = 2 * (4 * K * F * J + F * D * J)


def tile_attend_nsa_compress_pl_kernel(tc, tok_words, tok_scales, w0, w1, w2, w3, gain, wo,
                                            offs, offs2, offs3, offs4, out_0, out_1, out_2):
    nc = tc.nc
    with ExitStack() as ctx:
        keep = ctx.enter_context(tc.tile_pool(name="keep", bufs=1))
        psum = ctx.enter_context(tc.psum_pool(name="psum", bufs=1))

        def load_piece(name, w, c0, c1):
            raw = keep.tile([P, PACK, c1 - c0], F32, name="%s_raw%d" % (name, c0), tag="%s_raw%d" % (name, c0),
                            align_bytes=64)
            nc.sync.dma_start(out=raw[:], in_=w.rearrange("(p j) c -> p j c", j=PACK)[:, :, c0:c1])
            return raw, c0, c1

        def deal(copy, grouped, piece, c0=None, c1=None):
            raw, first, last = piece
            c0 = first if c0 is None else c0
            c1 = last if c1 is None else c1
            copy(out=grouped[:].rearrange("p (t m j) -> p m j t", t=PACK, j=PACK)[:, c0 // PACK:c1 // PACK],
                 in_=raw[:, :, c0 - first:c1 - first].rearrange("p j (m t) -> p m j t", t=PACK))

        def mx_tiles(name, n):
            codes = keep.tile([P, n], U32, name=name + "_codes", align_bytes=64)
            scales = keep.tile([P, n], U8, name=name + "_scales", align_bytes=64)
            return codes, scales

        def quantize(codes, scales, grouped):
            nc.vector.quantize_mx(out=codes.bitcast(FP8X4), scales=scales, in_=grouped)

        def interleave(grouped, rows):
            nc.vector.tensor_copy(out=grouped.rearrange("p (c i t) -> p c t i", i=4, t=PACK),
                                  in_=rows.rearrange("p t (c i) -> p c t i", i=4))

        pool_scales = keep.tile([P, T], U8, name="pool_scales", align_bytes=64)
        warm_in = keep.tile([P, 1], F32, name="warm_in")
        warm_out = keep.tile([P, 1], F32, name="warm_out")
        lists = [keep.tile([P, J // 16], U16, name="list%d" % i) for i in range(4)]
        pool_words = keep.tile([P, T], U32, name="pool_words", align_bytes=64)
        gain_sb = keep.tile([P, PACK], F32, name="gain_sb")

        nc.vector.memset(pool_scales[:].bitcast(I32), 0)
        raws = {}
        w0_raw = keep.tile([P, PACK, F], F32, name="w0_raw", align_bytes=64)
        w0_rows = w0.rearrange("(p j) c -> p j c", j=PACK)
        nc.sync.dma_start(out=w0_raw[:, 0, :], in_=w0_rows[:, 0, :])
        nc.sync.dma_start(lists[0][:], offs)
        nc.sync.dma_start(lists[1][:], offs2)
        for q in (0, 2, 1, 3):
            nc.sync.dma_start(out=pool_scales[32 * q:32 * q + 4, :].bitcast(I32),
                              in_=tok_scales[0, 4 * q:4 * q + 4, :].bitcast(I32))
        nc.sync.dma_start(out=w0_raw[:, 1:, :], in_=w0_rows[:, 1:, :])
        raws[0] = [(w0_raw, 0, F)]
        nc.sync.dma_start(lists[2][:], offs3)
        nc.sync.dma_start(lists[3][:], offs4)
        nc.sync.dma_start(out=pool_words[:].bitcast(I32),
                          in_=tok_words[0].rearrange("p n t -> p (n t)").bitcast(I32))
        raws[1] = [load_piece("w1", w1, 0, F)]
        raws[2] = [load_piece("w2", w2, 0, F)]
        raws[3] = [load_piece("w3", w3, 0, HALF), load_piece("w3", w3, HALF, F)]
        wo_raws = [load_piece("wo", wo, 0, D - P), load_piece("wo", wo, D - P, D)]
        nc.sync.dma_start(out=gain_sb[:], in_=gain.rearrange("(p t) o -> p (t o)", t=PACK))

        nc.vector.memset(warm_in[:], 0.0)
        nc.scalar.activation(out=warm_out[:], in_=warm_in[:], func=GELU)
        tok_s = []
        for i in range(4):
            s = keep.tile([P, J], U8, name="tok_s%d" % i, align_bytes=64)
            nc.vector.tensor_copy(out=s[:], in_=pool_scales[:].indirect(lists[i][:]))
            tok_s.append(s)

        z = [psum.tile([P, PACK, CH], F32, name="z%d" % c, tag="bank%d" % c) for c in range(NCH)]
        tok_w = []

        def gather_words(i, tag):
            g = keep.tile([P, J], U32, name="tok_w%d" % i, tag=tag, align_bytes=64)
            nc.vector.tensor_copy(out=g[:], in_=pool_words[:].indirect(lists[i][:]))
            tok_w.append(g)

        def first_layer(i, codes, scales, c, t):
            cols = slice(t * P, (t + 1) * P)
            js = slice(c * CH, (c + 1) * CH)
            nc.tensor.matmul_mx(out=z[c][:, t, :], lhsT=codes[:, cols].bitcast(FP8X4),
                                lhsT_scale=scales[:, cols], rhs=tok_w[i][:, js].bitcast(FP8X4),
                                rhs_scale=tok_s[i][:, js], start=(i == 0 and t == 0),
                                stop=(i == 3 and t == PACK - 1))

        width = F * PACK
        for i in range(3):
            gather_words(i, "tok_w%d" % i)
        for i in range(4):
            codes, scales = mx_tiles("w%d" % i, F)
            grouped = keep.tile([P, width], BF16, name="w%d_bf" % i, tag="w%d_bf" % i, align_bytes=64)
            deal(nc.scalar.copy, grouped, raws[i][0])
            if i == 3:
                deal(nc.scalar.copy, grouped, raws[i][1], HALF, W3_SPLIT)
                deal(nc.vector.tensor_copy, grouped, raws[i][1], W3_SPLIT, F)
            if i < 3:
                quantize(codes[:], scales[:], grouped[:])
            else:
                quantize(codes[:, :F // 2], scales[:, :F // 2], grouped[:, :width // 2])
                quantize(codes[:, F // 2:], scales[:, F // 2:], grouped[:, width // 2:])
            if i == 1:
                gather_words(3, "w1_raw0")
            if i < 3:
                for c in range(NCH):
                    for t in range(PACK):
                        first_layer(i, codes, scales, c, t)
            else:
                for cs in ((0, 1), (2, 3)):
                    for ts in ((0, 1), (2, 3)):
                        for c in cs:
                            for t in ts:
                                first_layer(i, codes, scales, c, t)

        wo_bf = keep.tile([P, width], BF16, name="wo_bf", align_bytes=64)
        deal(nc.scalar.copy, wo_bf, wo_raws[0], 0, HALF)
        wo_codes, wo_scales = mx_tiles("wo", D)

        def quantize_wo_half(h):
            for t in range(PACK):
                c0 = t * P + h * P // 2
                quantize(wo_codes[:, c0:c0 + P // 2], wo_scales[:, c0:c0 + P // 2],
                         wo_bf[:, c0 * PACK:(c0 + P // 2) * PACK])

        deal(nc.vector.tensor_copy, wo_bf, wo_raws[0], HALF, D - P)
        deal(nc.vector.tensor_copy, wo_bf, wo_raws[1])
        quantize_wo_half(0)
        quantize_wo_half(1)

        ybanks = [psum.tile([P, PACK, CH], F32, name="ybank%d" % c, tag="bank%d" % (NCH + c)) for c in range(NCH)]
        for u in range(SPARE):
            nc.tensor.matmul_mx(out=ybanks[NCH - 1][:].rearrange("p t j -> p (t j)"),
                                lhsT=codes[:, F - P:].bitcast(FP8X4), lhsT_scale=scales[:, F - P:],
                                rhs=codes[:].bitcast(FP8X4), rhs_scale=scales[:], start=True, stop=True)

        acts = []
        act_all = keep.tile([P, J * PACK], F32, name="act_all", align_bytes=64)
        for c in range(NCH):
            act = act_all[:, c * CH * PACK:(c + 1) * CH * PACK]
            act = act.rearrange("p (j t) -> p j t", t=PACK)
            nc.scalar.activation(out=act, in_=z[c][:].rearrange("p t j -> p j t"), func=GELU)
            acts.append(act)

        hidden = []
        for c in range(NCH):
            g_bf = keep.tile([P, CH * PACK], BF16, name="g_bf%d" % c, align_bytes=64)
            nc.vector.tensor_tensor(out=g_bf[:].rearrange("p (j t) -> p j t", t=PACK), in0=acts[c],
                                    in1=gain_sb[:].unsqueeze(1).to_broadcast([P, CH, PACK]), op=MULT)
            g_codes, g_scales = mx_tiles("g%d" % c, CH)
            quantize(g_codes[:], g_scales[:], g_bf[:])
            hidden.append((g_codes, g_scales))

        y_codes, y_scales = mx_tiles("y", J)
        out_rows = out_0.rearrange("(p t) j -> p t j", t=PACK)
        out_words = out_1[0].rearrange("p n t -> p (n t)").bitcast(I32)
        pair = 2 * CH
        for u in range(NCH // 2):
            y = keep.tile([P, PACK, pair], F32, name="y%d" % u, align_bytes=64)
            y_bf = keep.tile([P, pair * PACK], BF16, name="y_bf%d" % u, align_bytes=64)
            for e in range(2):
                c = 2 * u + e
                g_codes, g_scales = hidden[c]
                for t in range(PACK):
                    cols = slice(t * P, (t + 1) * P)
                    nc.tensor.matmul_mx(out=ybanks[c][:, t, :], lhsT=wo_codes[:, cols].bitcast(FP8X4),
                                        lhsT_scale=wo_scales[:, cols], rhs=g_codes[:].bitcast(FP8X4),
                                        rhs_scale=g_scales[:], start=True, stop=True)
                nc.scalar.copy(out=y[:, :, e * CH:(e + 1) * CH], in_=ybanks[c][:])
                nc.sync.dma_start(out=out_rows[:, :, c * CH:(c + 1) * CH], in_=y[:, :, e * CH:(e + 1) * CH])
                if c == NCH - 1:
                    nc.scalar.copy(out=y_bf[:, CH * PACK:].rearrange("p (j t) -> p j t", t=PACK),
                                   in_=ybanks[c][:].rearrange("p t j -> p j t"))
                if c < NCH - 1:
                    interleave(y_bf[:, e * CH * PACK:(e + 1) * CH * PACK], y[:, :, e * CH:(e + 1) * CH])
            js = slice(u * pair, (u + 1) * pair)
            if u == 0:
                quantize(y_codes[:, js], y_scales[:, js], y_bf[:])
            else:
                for e in range(2):
                    cj = slice(u * pair + e * CH, u * pair + (e + 1) * CH)
                    quantize(y_codes[:, cj], y_scales[:, cj], y_bf[:, e * CH * PACK:(e + 1) * CH * PACK])
            nc.sync.dma_start(out=out_words[:, js], in_=y_codes[:, js].bitcast(I32))
        for q in range(4):
            queue = nc.sync if q == 0 else nc.scalar
            queue.dma_start(out=out_2[0, 4 * q:4 * q + 4, :].bitcast(I32),
                            in_=y_scales[32 * q:32 * q + 4, :].bitcast(I32))
